import numpy as np
import ml_dtypes


def mxq(x, axis, fmt="e4m3"):
    dtype, down = {"e4m3": (ml_dtypes.float8_e4m3fn, 7), "e5m2": (ml_dtypes.float8_e5m2, 14)}[fmt]
    v = np.moveaxis(np.asarray(x, np.float32).astype(ml_dtypes.bfloat16).astype(np.float64), axis, -1)
    blocks = v.reshape(v.shape[:-1] + (-1, 32))
    amax = np.abs(blocks).max(-1, keepdims=True)
    byte = np.maximum(np.where(amax > 0, np.frexp(amax)[1] - 1 + 127, 0) - down, 1)
    scale = np.exp2(byte - 127.0)
    codes = (blocks / scale).astype(np.float32).astype(dtype).astype(np.float64)
    return np.moveaxis((codes * scale).reshape(v.shape), -1, axis)


WIDE = False


def mx_kscale(k):
    if not WIDE:
        return np.ones(k)
    levels = np.array([10, -10, 5, -5, 0])
    if k % 512:
        return np.exp2(np.random.permutation(np.resize(levels, k // 32))).repeat(32)
    a = np.empty((k // 512, 16))
    for p in range(k // 512):
        a[p, :8] = np.random.permutation(np.resize(levels, 8))
        for g in range(8):
            far = levels[np.abs(levels - a[p, g]) >= 10]
            a[p, g + 8] = far[np.random.randint(len(far))]
    return np.exp2(a.ravel()).repeat(32)


def f64(x):
    return np.asarray(x).astype(np.float64)


def striped(idx):
    return np.tile(idx.reshape(-1, 16).T, (8, 1)).astype(np.uint16)


def unstriped(offs):
    return offs[:16].T.reshape(-1).astype(np.int64)


def striped8(idx):
    return np.concatenate([x.reshape(-1, 16).T for x in idx]).astype(np.uint16)


def runs(offs, k):
    lists = np.stack([offs[16 * r : 16 * r + 16].T.reshape(-1) for r in range(8)]).astype(np.int64)
    return lists[np.arange(k) % 512 // 64]


def pack_weight(w):
    k, n = w.shape
    w = f64(np.asarray(w, np.float32).astype(ml_dtypes.bfloat16)).reshape(k // 32, 32, n)
    amax = np.abs(w).max(1)
    byte = np.clip(np.where(amax > 0, np.frexp(amax)[1] - 1 + 127 - 7, 1), 1, 254)
    scaled = (w * np.exp2(127.0 - byte)[:, None, :]).reshape(k, n).astype(np.float32)
    words = np.ascontiguousarray(scaled.reshape(k // 512, 128, 4, n).transpose(0, 1, 3, 2)).astype(ml_dtypes.float8_e4m3fn).view(np.uint8)
    return words, np.ascontiguousarray(byte.astype(np.uint8).reshape(k // 512, 16, n))


def unpack_weight(words, scales):
    g, p, n, _ = words.shape
    vals = np.ascontiguousarray(words).view(ml_dtypes.float8_e4m3fn).astype(np.float64) * np.repeat(np.exp2(scales.astype(np.float64) - 127.0), 8, axis=1)[..., None]
    return vals.transpose(0, 1, 3, 2).reshape(g * 512, n)


K, T, S, N, H, W, U = 512, 2048, 512, 512, 512, 256, 1024


def setup_inputs():
    n = np.random.standard_normal
    s = mx_kscale(K)[:, None]
    u = mx_kscale(H)
    packed_xT = pack_weight(n((K, T)) * s)
    perm = np.stack([np.random.permutation(S) for _ in range(8)])
    return {
        "x_words": packed_xT[0],
        "x_scales": packed_xT[1],
        "w1": (n((K, H)) / np.sqrt(K) / s * u).astype(np.float32),
        "w2": (n((H, H)) / np.sqrt(H) / u[:, None] * u).astype(np.float32),
        "mem": (n((H, U)) * u[:, None]).astype(np.float32),
        "w3": (n((H, N)) / np.sqrt(H) / u[:, None]).astype(np.float32),
        "res": n((N, U)).astype(np.float32),
        "offs": striped(np.random.permutation(T)[:S]),
        "n1": striped8(perm[:, :W]),
        "n2": striped8(perm[:, W:]),
        "n3": striped8(np.stack([np.random.permutation(U)[:S] for _ in range(8)])),
        "n4": striped8(np.stack([np.random.permutation(U) for _ in range(8)])),
    }


def reference(x_words, x_scales, w1, w2, mem, w3, res, offs, n1, n2, n3, n4):
    xq = unpack_weight(x_words, x_scales)[:, unstriped(offs)]
    y = mxq(f64(w1), 0, "e4m3").T @ xq
    pa = y[np.arange(H)[:, None], runs(n1, H)]
    pb = y[np.arange(H)[:, None], runs(n2, H)]
    rb = np.minimum(pa, pb)
    ra = np.maximum(pa, pb)
    ds = np.zeros((H, S))
    ds[np.arange(H)[:, None], runs(n1, H)] = ra
    z = ds.copy()
    z[np.arange(H)[:, None], runs(n2, H)] = rb
    h = mxq(f64(w2), 0, "e4m3").T @ mxq(z, 0, "e4m3")
    pg = f64(mem).copy()
    pg[np.arange(H)[:, None], runs(n3, H)] = h
    z2 = pg - (0.5 * (pg[np.arange(H)[:, None], runs(n4, H)]))
    return f64(res) + (mxq(f64(w3), 0, "e4m3").T @ mxq(z2, 0, "e4m3"))

@@ -1,0 +1,264 @@
+from contextlib import ExitStack
+
+import concourse.mybir as mybir
+
+K, T, S, N, H, W, U = 512, 2048, 512, 512, 512, 256, 1024
+FLOPS = 2 * K * H * S + 2 * H * H * S + 2 * H * N * U
+
+F32 = mybir.dt.float32
+BF16 = mybir.dt.bfloat16
+I32 = mybir.dt.int32
+U32 = mybir.dt.uint32
+U16 = mybir.dt.uint16
+U8 = mybir.dt.uint8
+FP8X4 = mybir.dt.float8_e4m3fn_x4
+ALU = mybir.AluOpType
+COPY = mybir.ActivationFunctionType.Copy
+
+P = 128
+PACK = 4
+LANES = 16
+CH = 128
+CW = 256
+M_SPLIT = 80
+
+
+def tile_picked_deeporderpagem_none_p_kernel(
+    tc, x_words, x_scales, w1, w2, mem, w3, res, offs, n1, n2, n3, n4, out
+):
+    nc = tc.nc
+    with ExitStack() as ctx:
+        keep = ctx.enter_context(tc.tile_pool(name="keep", bufs=1))
+        psum = ctx.enter_context(tc.psum_pool(name="psum", bufs=8))
+
+        def sb(name, shape, dtype, tag=None):
+            return keep.tile(shape, dtype, name=name, tag=tag or name, align_bytes=64)
+
+        def bank(name):
+            return psum.tile([P, 512], F32, name=name, tag="bank")
+
+        def load_list(name, src):
+            tile = keep.tile(list(src.shape), U16, name=name, tag=name)
+            nc.sync.dma_start(tile[:], src)
+            return tile
+
+        def load_weight(name, src):
+            raw = sb(name, [P, PACK, 512], F32)
+            nc.sync.dma_start(raw[:], src.rearrange("(p j) c -> p j c", j=PACK))
+            return raw
+
+        def quantize(codes, scales, values):
+            nc.vector.quantize_mx(out=codes.bitcast(FP8X4), scales=scales, in_=values)
+
+        def mx(dst, lhs, lhs_cols, rhs, rhs_cols):
+            nc.tensor.matmul_mx(
+                out=dst,
+                lhsT=lhs[0][:, lhs_cols].bitcast(FP8X4),
+                lhsT_scale=lhs[1][:, lhs_cols],
+                rhs=rhs[0][:, rhs_cols].bitcast(FP8X4),
+                rhs_scale=rhs[1][:, rhs_cols],
+                start=True,
+                stop=True,
+            )
+
+        def dealt(grouped, raw, m0, m1, base=0):
+            dst = grouped[:].rearrange("p (t m j) -> p m t j", t=PACK, j=PACK)[:, m0:m1]
+            src = raw[:].rearrange("p j (m t) -> p m t j", t=PACK)[:, m0 - base : m1 - base]
+            return dst, src
+
+        xs = sb("xs", [P, T], U8)
+        nc.vector.memset(xs[:].bitcast(I32), 0)
+        offs_t = load_list("offs_t", offs)
+        n1_t = load_list("n1_t", n1)
+        n2_t = load_list("n2_t", n2)
+        n3_t = load_list("n3_t", n3)
+        w1_v = w1.rearrange("(p j) c -> p j c", j=PACK)
+        w1_raw = []
+        for half in range(2):
+            raw = sb(f"w1_raw{half}", [P, PACK, H // 2], F32)
+            nc.sync.dma_start(raw[:], w1_v[:, :, half * (H // 2) : (half + 1) * (H // 2)])
+            w1_raw.append(raw)
+        xw = sb("xw", [P, T], U32)
+        nc.sync.dma_start(xw[:].bitcast(I32), x_words[0].rearrange("p n r -> p (n r)").bitcast(I32))
+        n4_t = load_list("n4_t", n4)
+        for q in range(4):
+            nc.scalar.dma_start(
+                xs[32 * q : 32 * q + 4, :].bitcast(I32), x_scales[0, 4 * q : 4 * q + 4, :].bitcast(I32)
+            )
+        w2_raw = load_weight("w2_raw", w2)
+        w3_raw = load_weight("w3_raw", w3)
+        mem_v = mem.rearrange("(p t) u -> p t u", t=PACK)
+        page = []
+        for t in range(PACK):
+            pg = sb(f"page{t}", [P, U], F32)
+            nc.sync.dma_start(pg[:], mem_v[:, t, :])
+            page.append(pg)
+        res_v = res.rearrange("(b p) u -> p b u", p=P)
+        out_v = out.rearrange("(b p) u -> p b u", p=P)
+        res_t = []
+        for c in range(U // CW):
+            r = sb(f"res{c}", [P, PACK, CW], F32)
+            nc.sync.dma_start(r[:], res_v[:, :, c * CW : (c + 1) * CW])
+            res_t.append(r)
+
+        x_sc = sb("x_sc", [P, S], U8)
+        nc.vector.tensor_copy(x_sc[:], xs[:].indirect(offs_t[:]))
+        w1_bf = sb("w1_bf", [P, PACK * H], BF16)
+        nc.scalar.copy(*dealt(w1_bf, w1_raw[0], 0, P // 2))
+        nc.scalar.copy(*dealt(w1_bf, w1_raw[1], P // 2, M_SPLIT, P // 2))
+        nc.vector.tensor_copy(*dealt(w1_bf, w1_raw[1], M_SPLIT, P, P // 2))
+        w1_q = (sb("w1_codes", [P, H], U32), sb("w1_scales", [P, H], U8))
+        for c0, c1 in ((0, P), (P, 2 * P), (2 * P, H)):
+            quantize(w1_q[0][:, c0:c1], w1_q[1][:, c0:c1], w1_bf[:, PACK * c0 : PACK * c1])
+        x_cd = sb("x_cd", [P, S], U32)
+        x_q = (x_cd, x_sc)
+        y = [sb(f"y{t}", [P, S], F32) for t in range(PACK)]
+        for half in range(2):
+            cols = slice(half * W, (half + 1) * W)
+            nc.vector.tensor_copy(x_cd[:, cols], xw[:].indirect(offs_t[:, half * W // LANES : (half + 1) * W // LANES]))
+            acc = bank(f"y0_ps{half}")
+            mx(acc[:, 0:W], w1_q, slice(0, P), x_q, cols)
+            nc.scalar.copy(y[0][:, cols], acc[:, 0:W])
+        for t in range(1, PACK):
+            acc = bank(f"y_ps{t}")
+            mx(acc[:], w1_q, slice(t * P, (t + 1) * P), x_q, slice(0, S))
+            nc.scalar.copy(y[t][:], acc[:])
+
+        w2_bf = sb("w2_bf", [P, PACK * H], BF16)
+        nc.scalar.copy(*dealt(w2_bf, w2_raw, 0, P))
+        w3_bf = sb("w3_bf", [P, PACK * N], BF16)
+        nc.scalar.copy(
+            w3_bf[:].rearrange("p (c i j) -> p c j i", i=4, j=PACK),
+            w3_raw[:].rearrange("p j (c i) -> p c j i", i=4),
+        )
+
+        last = PACK - 1
+        pair = [sb(f"pair{t}", [P, 2, W], F32, tag="hold_w2" if t == last else None) for t in range(PACK)]
+        high = [sb(f"high{t}", [P, W], F32) for t in range(PACK)]
+        low = [sb(f"low{t}", [P, W], F32, tag="hold_w3" if t == last else None) for t in range(PACK)]
+        z = [sb(f"z{t}", [P, S], F32) for t in range(PACK)]
+        z_bf = sb("z_bf", [P, S, PACK], BF16)
+
+        def fetch(t, side):
+            if t < PACK:
+                nc.vector.tensor_copy(pair[t][:, side, :], y[t][:].indirect((n1_t, n2_t)[side][:]))
+
+        def larger(t):
+            if t < PACK:
+                nc.vector.tensor_tensor(high[t][:], pair[t][:, 0, :], pair[t][:, 1, :], ALU.max)
+
+        def smaller(t):
+            if t < PACK:
+                nc.vector.tensor_tensor(low[t][:], pair[t][:, 0, :], pair[t][:, 1, :], ALU.min)
+
+        fetch(0, 0)
+        fetch(0, 1)
+        fetch(1, 0)
+        larger(0)
+        smaller(0)
+        fetch(1, 1)
+        for t in range(PACK):
+            nc.vector.tensor_copy(z[t][:].indirect(n1_t[:]), high[t][:])
+            fetch(t + 2, 0)
+            larger(t + 1)
+            nc.vector.tensor_copy(z[t][:].indirect(n2_t[:]), low[t][:])
+            fetch(t + 2, 1)
+            smaller(t + 1)
+            if t < last:
+                nc.scalar.copy(z_bf[:, :, t], z[t][:])
+
+        w2_q = (sb("w2_codes", [P, H], U32, tag="hold_w2"), sb("w2_scales", [P, H], U8))
+        quantize(w2_q[0][:], w2_q[1][:], w2_bf[:])
+        w3_q = (sb("w3_codes", [P, N], U32, tag="hold_w3"), sb("w3_scales", [P, N], U8))
+
+        z_q = (sb("z_codes", [P, S], U32), sb("z_scales", [P, S], U8))
+
+        def round_last(c0, c1):
+            nc.scalar.copy(z_bf[:, c0:c1, last], z[last][:, c0:c1])
+
+        def quantize_z(c0, c1):
+            quantize(z_q[0][:, c0:c1], z_q[1][:, c0:c1], z_bf[:, c0:c1, :].rearrange("p c t -> p (c t)"))
+
+        round_last(0, CH)
+        quantize_z(0, CH)
+        quantize(w3_q[0][:], w3_q[1][:], w3_bf[:])
+        round_last(CH, 2 * CH)
+        h_first = []
+        for t in range(PACK):
+            acc = bank(f"hf_ps{t}")
+            mx(acc[:, 0:CH], w2_q, slice(t * P, (t + 1) * P), z_q, slice(0, CH))
+            ht = sb(f"h_first{t}", [P, CH], F32)
+            nc.scalar.copy(ht[:], acc[:, 0:CH])
+            h_first.append(ht)
+        round_last(2 * CH, 3 * CH)
+        round_last(3 * CH, 4 * CH)
+
+        def put(t, c0, c1, src):
+            nc.vector.tensor_copy(page[t][:].indirect(n3_t[:, c0 // LANES : c1 // LANES]), src)
+
+        put(0, 0, CH, h_first[0][:])
+        quantize_z(CH, 2 * CH)
+        put(1, 0, CH, h_first[1][:])
+        quantize_z(2 * CH, S)
+        put(2, 0, CH, h_first[2][:])
+        put(3, 0, CH, h_first[3][:])
+        h_rest = []
+        for t in range(PACK):
+            acc = bank(f"hr_ps{t}")
+            mx(acc[:, CH : 2 * CH], w2_q, slice(t * P, (t + 1) * P), z_q, slice(CH, 2 * CH))
+            mx(acc[:, 2 * CH : S], w2_q, slice(t * P, (t + 1) * P), z_q, slice(2 * CH, S))
+            ht = sb(f"h_rest{t}", [P, S - CH], F32)
+            nc.scalar.copy(ht[:], acc[:, CH:S])
+            h_rest.append(ht)
+        twice = [sb(f"twice{t}", [P, U], F32) for t in range(PACK)]
+        for t in range(PACK):
+            put(t, CH, S, h_rest[t][:])
+            for c in range(U // CW):
+                cols = slice(c * CW, (c + 1) * CW)
+                nc.scalar.activation(twice[t][:, cols], page[t][:, cols], COPY, scale=2.0)
+
+        chunks = U // CW
+        diff = [sb(f"diff{c}", [P, PACK, CW], F32) for c in range(chunks)]
+        z2_q = [None] * chunks
+
+        def fetch_diff(c):
+            cols = slice(c * CW, (c + 1) * CW)
+            for t in range(PACK):
+                nc.vector.tensor_tensor(
+                    diff[c][:, t, :],
+                    page[t][:].indirect(n4_t[:, c * CW // LANES : (c + 1) * CW // LANES]),
+                    twice[t][:, cols],
+                    ALU.subtract,
+                )
+
+        def quantize_z2(c):
+            z2_bf = sb(f"z2_bf{c}", [P, CW * PACK], BF16)
+            nc.scalar.activation(
+                z2_bf[:].rearrange("p (c i t) -> p c t i", i=4, t=PACK),
+                diff[c][:].rearrange("p t (c i) -> p c t i", i=4),
+                COPY,
+                scale=-0.5,
+            )
+            z2_q[c] = (sb(f"z2_codes{c}", [P, CW], U32), sb(f"z2_scales{c}", [P, CW], U8))
+            quantize(z2_q[c][0][:], z2_q[c][1][:], z2_bf[:])
+
+        def finish(c):
+            for half in range(2):
+                acc = bank(f"o_ps{c}_{half}")
+                for i in range(2):
+                    b = 2 * half + i
+                    mx(acc[:, i * CW : (i + 1) * CW], w3_q, slice(b * P, (b + 1) * P), z2_q[c], slice(0, CW))
+                rows = slice(2 * half, 2 * half + 2)
+                done = sb(f"done{c}_{half}", [P, 2, CW], F32)
+                nc.vector.tensor_tensor(
+                    done[:], acc[:].rearrange("p (b w) -> p b w", b=2), res_t[c][:, rows, :], ALU.add
+                )
+                nc.sync.dma_start(out_v[:, rows, c * CW : (c + 1) * CW], done[:])
+
+        for step in range(chunks + 2):
+            if step < chunks:
+                fetch_diff(step)
+            if 1 <= step <= chunks:
+                quantize_z2(step - 1)
+            if step >= 2:
+                finish(step - 2)

@@ -1,6 +1,7 @@
 from contextlib import ExitStack
 
 import concourse.mybir as mybir
+from concourse.masks import make_identity
 
 K, T, S, N, H, W, U = 512, 2048, 512, 512, 512, 256, 1024
 FLOPS = 2 * K * H * S + 2 * H * H * S + 2 * H * N * U
@@ -29,13 +30,13 @@ def tile_picked_deeporderpagem_none_p_kernel(
     nc = tc.nc
     with ExitStack() as ctx:
         keep = ctx.enter_context(tc.tile_pool(name="keep", bufs=1))
-        psum = ctx.enter_context(tc.psum_pool(name="psum", bufs=8))
+        psum = ctx.enter_context(tc.psum_pool(name="psum", bufs=1))
 
         def sb(name, shape, dtype, tag=None):
             return keep.tile(shape, dtype, name=name, tag=tag or name, align_bytes=64)
 
-        def bank(name):
-            return psum.tile([P, 512], F32, name=name, tag="bank")
+        def bank(name, number):
+            return psum.tile([P, 512], F32, name=name, tag=f"bank{number}")
 
         def load_list(name, src):
             tile = keep.tile(list(src.shape), U16, name=name, tag=name)
@@ -87,19 +88,27 @@ def tile_picked_deeporderpagem_none_p_kernel(
             )
         w2_raw = load_weight("w2_raw", w2)
         w3_raw = load_weight("w3_raw", w3)
+        res_v = res.rearrange("(b p) u -> p b u", p=P)
+        out_v = out.rearrange("(b p) u -> p b u", p=P)
+
+        def load_res(c):
+            halves = []
+            for half in range(2):
+                r = sb(f"res{c}_{half}", [P, 2, CW], F32)
+                nc.sync.dma_start(r[:], res_v[:, 2 * half : 2 * half + 2, c * CW : (c + 1) * CW])
+                halves.append(r)
+            return halves
+
+        res_t = [load_res(0)]
         mem_v = mem.rearrange("(p t) u -> p t u", t=PACK)
         page = []
         for t in range(PACK):
             pg = sb(f"page{t}", [P, U], F32)
             nc.sync.dma_start(pg[:], mem_v[:, t, :])
             page.append(pg)
-        res_v = res.rearrange("(b p) u -> p b u", p=P)
-        out_v = out.rearrange("(b p) u -> p b u", p=P)
-        res_t = []
-        for c in range(U // CW):
-            r = sb(f"res{c}", [P, PACK, CW], F32)
-            nc.sync.dma_start(r[:], res_v[:, :, c * CW : (c + 1) * CW])
-            res_t.append(r)
+        res_t.extend(load_res(c) for c in range(1, U // CW))
+        ident = sb("ident", [P, P], F32)
+        make_identity(nc, ident[:])
 
         x_sc = sb("x_sc", [P, S], U8)
         nc.vector.tensor_copy(x_sc[:], xs[:].indirect(offs_t[:]))
@@ -116,11 +125,11 @@ def tile_picked_deeporderpagem_none_p_kernel(
         for half in range(2):
             cols = slice(half * W, (half + 1) * W)
             nc.vector.tensor_copy(x_cd[:, cols], xw[:].indirect(offs_t[:, half * W // LANES : (half + 1) * W // LANES]))
-            acc = bank(f"y0_ps{half}")
+            acc = bank(f"y0_ps{half}", half)
             mx(acc[:, 0:W], w1_q, slice(0, P), x_q, cols)
             nc.scalar.copy(y[0][:, cols], acc[:, 0:W])
         for t in range(1, PACK):
-            acc = bank(f"y_ps{t}")
+            acc = bank(f"y_ps{t}", t + 1)
             mx(acc[:], w1_q, slice(t * P, (t + 1) * P), x_q, slice(0, S))
             nc.scalar.copy(y[t][:], acc[:])
 
@@ -132,44 +141,64 @@ def tile_picked_deeporderpagem_none_p_kernel(
             w3_raw[:].rearrange("p j (c i) -> p c j i", i=4),
         )
 
+        totals = []
+        for wb in range(CW // P):
+            acc = bank(f"rt_ps{wb}", 4 + wb)
+            for b in range(PACK):
+                nc.tensor.transpose(
+                    acc[:, b * P : (b + 1) * P], res_t[0][b // 2][:, b % 2, wb * P : (wb + 1) * P], ident[:]
+                )
+            turned = sb(f"res_turned{wb}", [P, N], F32)
+            nc.scalar.copy(turned[:], acc[:])
+            total = bank(f"os_ps{wb}", 6 + wb)
+            for b in range(PACK):
+                rows = slice(b * P, (b + 1) * P)
+                nc.tensor.matmul(total[:, rows], turned[:, rows], ident[:], start=b == 0, stop=False, is_transpose=True)
+            totals.append(total)
+
         last = PACK - 1
-        pair = [sb(f"pair{t}", [P, 2, W], F32, tag="hold_w2" if t == last else None) for t in range(PACK)]
-        high = [sb(f"high{t}", [P, W], F32) for t in range(PACK)]
-        low = [sb(f"low{t}", [P, W], F32, tag="hold_w3" if t == last else None) for t in range(PACK)]
+        pair = [sb(f"pair{g}", [P, 2, 2, W], F32) for g in range(2)]
+        high = [sb(f"high{g}", [P, 2, W], F32) for g in range(2)]
+        low = [sb(f"low{g}", [P, 2, W], F32) for g in range(2)]
         z = [sb(f"z{t}", [P, S], F32) for t in range(PACK)]
         z_bf = sb("z_bf", [P, S, PACK], BF16)
 
         def fetch(t, side):
-            if t < PACK:
-                nc.vector.tensor_copy(pair[t][:, side, :], y[t][:].indirect((n1_t, n2_t)[side][:]))
+            nc.vector.tensor_copy(pair[t // 2][:, side, t % 2, :], y[t][:].indirect((n1_t, n2_t)[side][:]))
 
-        def larger(t):
-            if t < PACK:
-                nc.vector.tensor_tensor(high[t][:], pair[t][:, 0, :], pair[t][:, 1, :], ALU.max)
+        def order(g):
+            nc.vector.tensor_tensor(high[g][:], pair[g][:, 0], pair[g][:, 1], ALU.max)
+            nc.vector.tensor_tensor(low[g][:], pair[g][:, 0], pair[g][:, 1], ALU.min)
 
-        def smaller(t):
-            if t < PACK:
-                nc.vector.tensor_tensor(low[t][:], pair[t][:, 0, :], pair[t][:, 1, :], ALU.min)
+        def put_high(t):
+            nc.vector.tensor_copy(z[t][:].indirect(n1_t[:]), high[t // 2][:, t % 2, :])
 
-        fetch(0, 0)
-        fetch(0, 1)
-        fetch(1, 0)
-        larger(0)
-        smaller(0)
-        fetch(1, 1)
-        for t in range(PACK):
-            nc.vector.tensor_copy(z[t][:].indirect(n1_t[:]), high[t][:])
-            fetch(t + 2, 0)
-            larger(t + 1)
-            nc.vector.tensor_copy(z[t][:].indirect(n2_t[:]), low[t][:])
-            fetch(t + 2, 1)
-            smaller(t + 1)
+        def put_low(t):
+            nc.vector.tensor_copy(z[t][:].indirect(n2_t[:]), low[t // 2][:, t % 2, :])
             if t < last:
                 nc.scalar.copy(z_bf[:, :, t], z[t][:])
 
-        w2_q = (sb("w2_codes", [P, H], U32, tag="hold_w2"), sb("w2_scales", [P, H], U8))
+        for t in range(2):
+            fetch(t, 0)
+            fetch(t, 1)
+        fetch(2, 0)
+        order(0)
+        fetch(2, 1)
+        put_high(0)
+        fetch(3, 0)
+        put_low(0)
+        fetch(3, 1)
+        put_high(1)
+        order(1)
+        put_low(1)
+        put_high(2)
+        put_high(3)
+        put_low(2)
+        put_low(3)
+
+        w2_q = (sb("w2_codes", [P, H], U32, tag="high1"), sb("w2_scales", [P, H], U8))
         quantize(w2_q[0][:], w2_q[1][:], w2_bf[:])
-        w3_q = (sb("w3_codes", [P, N], U32, tag="hold_w3"), sb("w3_scales", [P, N], U8))
+        w3_q = (sb("w3_codes", [P, N], U32, tag="low1"), sb("w3_scales", [P, N], U8))
 
         z_q = (sb("z_codes", [P, S], U32), sb("z_scales", [P, S], U8))
 
@@ -185,7 +214,7 @@ def tile_picked_deeporderpagem_none_p_kernel(
         round_last(CH, 2 * CH)
         h_first = []
         for t in range(PACK):
-            acc = bank(f"hf_ps{t}")
+            acc = bank(f"hf_ps{t}", t)
             mx(acc[:, 0:CH], w2_q, slice(t * P, (t + 1) * P), z_q, slice(0, CH))
             ht = sb(f"h_first{t}", [P, CH], F32)
             nc.scalar.copy(ht[:], acc[:, 0:CH])
@@ -204,61 +233,85 @@ def tile_picked_deeporderpagem_none_p_kernel(
         put(3, 0, CH, h_first[3][:])
         h_rest = []
         for t in range(PACK):
-            acc = bank(f"hr_ps{t}")
+            acc = bank(f"hr_ps{t}", (4 + t) % 6)
             mx(acc[:, CH : 2 * CH], w2_q, slice(t * P, (t + 1) * P), z_q, slice(CH, 2 * CH))
             mx(acc[:, 2 * CH : S], w2_q, slice(t * P, (t + 1) * P), z_q, slice(2 * CH, S))
             ht = sb(f"h_rest{t}", [P, S - CH], F32)
             nc.scalar.copy(ht[:], acc[:, CH:S])
             h_rest.append(ht)
-        twice = [sb(f"twice{t}", [P, U], F32) for t in range(PACK)]
+        chunks = U // CW
+        twice = []
         for t in range(PACK):
             put(t, CH, S, h_rest[t][:])
-            for c in range(U // CW):
-                cols = slice(c * CW, (c + 1) * CW)
-                nc.scalar.activation(twice[t][:, cols], page[t][:, cols], COPY, scale=2.0)
+            parts = []
+            for c in range(chunks):
+                part = sb(f"twice{t}_{c}", [P, CW], F32)
+                nc.scalar.activation(part[:], page[t][:, c * CW : (c + 1) * CW], COPY, scale=2.0)
+                parts.append(part)
+            twice.append(parts)
 
-        chunks = U // CW
-        diff = [sb(f"diff{c}", [P, PACK, CW], F32) for c in range(chunks)]
+        diff = [None] * chunks
         z2_q = [None] * chunks
 
         def fetch_diff(c):
-            cols = slice(c * CW, (c + 1) * CW)
+            diff[c] = sb(f"diff{c}", [P, PACK, CW], F32, tag=("h_rest2", "twice3_0", "z2_bf0", "z2_bf1")[c])
             for t in range(PACK):
                 nc.vector.tensor_tensor(
                     diff[c][:, t, :],
                     page[t][:].indirect(n4_t[:, c * CW // LANES : (c + 1) * CW // LANES]),
-                    twice[t][:, cols],
+                    twice[t][c][:],
                     ALU.subtract,
                 )
 
         def quantize_z2(c):
-            z2_bf = sb(f"z2_bf{c}", [P, CW * PACK], BF16)
+            z2_bf = sb(f"z2_bf{c}", [P, CW * PACK], BF16, tag="prod_turned1" if c == 2 else None)
             nc.scalar.activation(
                 z2_bf[:].rearrange("p (c i t) -> p c t i", i=4, t=PACK),
                 diff[c][:].rearrange("p t (c i) -> p c t i", i=4),
                 COPY,
                 scale=-0.5,
             )
-            z2_q[c] = (sb(f"z2_codes{c}", [P, CW], U32), sb(f"z2_scales{c}", [P, CW], U8))
+            behind = f"twice2_{c + 1}" if c + 1 < chunks else None
+            z2_q[c] = (sb(f"z2_codes{c}", [P, CW], U32, tag=behind), sb(f"z2_scales{c}", [P, CW], U8))
             quantize(z2_q[c][0][:], z2_q[c][1][:], z2_bf[:])
 
         def finish(c):
+            first_behind = (None, "prod_turned1", "z2_bf3", None)[c]
             for half in range(2):
-                acc = bank(f"o_ps{c}_{half}")
+                acc = bank(f"o_ps{c}_{half}", (4 + 2 * c + half) % 8)
                 for i in range(2):
                     b = 2 * half + i
                     mx(acc[:, i * CW : (i + 1) * CW], w3_q, slice(b * P, (b + 1) * P), z2_q[c], slice(0, CW))
                 rows = slice(2 * half, 2 * half + 2)
-                done = sb(f"done{c}_{half}", [P, 2, CW], F32)
+                done = sb(f"done{c}_{half}", [P, 2, CW], F32, tag=first_behind if half == 0 else f"res{c}_0")
                 nc.vector.tensor_tensor(
-                    done[:], acc[:].rearrange("p (b w) -> p b w", b=2), res_t[c][:, rows, :], ALU.add
+                    done[:], acc[:].rearrange("p (b w) -> p b w", b=2), res_t[c][half][:], ALU.add
                 )
                 nc.sync.dma_start(out_v[:, rows, c * CW : (c + 1) * CW], done[:])
+
+        def finish_turned(c):
+            done = sb(f"done{c}", [P, PACK, CW], F32)
+            for wb in range(CW // P):
+                cols = slice(wb * P, (wb + 1) * P)
+                acc = bank(f"ot_ps{wb}", 2 + wb)
+                mx(acc[:], z2_q[c], cols, w3_q, slice(0, N))
+                prod = sb(f"prod_turned{wb}", [P, N], F32)
+                nc.scalar.copy(prod[:], acc[:])
+                total = totals[wb]
+                for b in range(PACK):
+                    rows = slice(b * P, (b + 1) * P)
+                    nc.tensor.matmul(
+                        total[:, rows], prod[:, rows], ident[:], start=False, stop=b == last, is_transpose=True
+                    )
+                nc.scalar.copy(done[:, :, cols], total[:].rearrange("p (b w) -> p b w", b=PACK))
+            nc.sync.dma_start(out_v[:, :, c * CW : (c + 1) * CW], done[:])
 
         for step in range(chunks + 2):
             if step < chunks:
                 fetch_diff(step)
             if 1 <= step <= chunks:
                 quantize_z2(step - 1)
-            if step >= 2:
+            if step == 1:
+                finish_turned(0)
+            if step >= 3:
                 finish(step - 2)

@@ -240,21 +240,25 @@ def tile_picked_deeporderpagem_none_p_kernel(
             nc.scalar.copy(ht[:], acc[:, CH:S])
             h_rest.append(ht)
         chunks = U // CW
-        twice = []
+        twice = [[sb(f"twice{t}_{c}", [P, CW], F32) for c in range(chunks)] for t in range(PACK)]
+
+        def double(t, c):
+            nc.scalar.activation(twice[t][c][:], page[t][:, c * CW : (c + 1) * CW], COPY, scale=2.0)
+
         for t in range(PACK):
             put(t, CH, S, h_rest[t][:])
-            parts = []
-            for c in range(chunks):
-                part = sb(f"twice{t}_{c}", [P, CW], F32)
-                nc.scalar.activation(part[:], page[t][:, c * CW : (c + 1) * CW], COPY, scale=2.0)
-                parts.append(part)
-            twice.append(parts)
+            if t < 2:
+                for c in range(chunks):
+                    double(t, c)
+        for c in range(chunks):
+            double(2, c)
+            double(3, c)
 
         diff = [None] * chunks
         z2_q = [None] * chunks
 
         def fetch_diff(c):
-            diff[c] = sb(f"diff{c}", [P, PACK, CW], F32, tag=("h_rest2", "twice3_0", "z2_bf0", "z2_bf1")[c])
+            diff[c] = sb(f"diff{c}", [P, PACK, CW], F32, tag=("h_rest2", "twice2_0")[c % 2])
             for t in range(PACK):
                 nc.vector.tensor_tensor(
                     diff[c][:, t, :],
@@ -276,18 +280,17 @@ def tile_picked_deeporderpagem_none_p_kernel(
             quantize(z2_q[c][0][:], z2_q[c][1][:], z2_bf[:])
 
         def finish(c):
-            first_behind = (None, "prod_turned1", "z2_bf3", None)[c]
+            done = sb(f"done{c}", [P, PACK, CW], F32, tag=(None, "h_rest2", "twice2_0", None)[c])
             for half in range(2):
                 acc = bank(f"o_ps{c}_{half}", (4 + 2 * c + half) % 8)
                 for i in range(2):
                     b = 2 * half + i
                     mx(acc[:, i * CW : (i + 1) * CW], w3_q, slice(b * P, (b + 1) * P), z2_q[c], slice(0, CW))
                 rows = slice(2 * half, 2 * half + 2)
-                done = sb(f"done{c}_{half}", [P, 2, CW], F32, tag=first_behind if half == 0 else f"res{c}_0")
                 nc.vector.tensor_tensor(
-                    done[:], acc[:].rearrange("p (b w) -> p b w", b=2), res_t[c][half][:], ALU.add
+                    done[:, rows, :], acc[:].rearrange("p (b w) -> p b w", b=2), res_t[c][half][:], ALU.add
                 )
-                nc.sync.dma_start(out_v[:, rows, c * CW : (c + 1) * CW], done[:])
+                nc.sync.dma_start(out_v[:, rows, c * CW : (c + 1) * CW], done[:, rows, :])
 
         def finish_turned(c):
             done = sb(f"done{c}", [P, PACK, CW], F32)

@@ -268,7 +268,7 @@ def tile_picked_deeporderpagem_none_p_kernel(
                 )
 
         def quantize_z2(c):
-            z2_bf = sb(f"z2_bf{c}", [P, CW * PACK], BF16, tag="prod_turned1" if c == 2 else None)
+            z2_bf = sb(f"z2_bf{c}", [P, CW * PACK], BF16, tag=(None, None, "twice2_1", "prod_turned0")[c])
             nc.scalar.activation(
                 z2_bf[:].rearrange("p (c i t) -> p c t i", i=4, t=PACK),
                 diff[c][:].rearrange("p t (c i) -> p c t i", i=4),
@@ -282,7 +282,7 @@ def tile_picked_deeporderpagem_none_p_kernel(
         def finish(c):
             done = sb(f"done{c}", [P, PACK, CW], F32, tag=(None, "h_rest2", "twice2_0", None)[c])
             for half in range(2):
-                acc = bank(f"o_ps{c}_{half}", (4 + 2 * c + half) % 8)
+                acc = bank(f"o_ps{c}_{half}", ((), (3, 2), (4, 5), (0, 1))[c][half])
                 for i in range(2):
                     b = 2 * half + i
                     mx(acc[:, i * CW : (i + 1) * CW], w3_q, slice(b * P, (b + 1) * P), z2_q[c], slice(0, CW))
@@ -292,8 +292,7 @@ def tile_picked_deeporderpagem_none_p_kernel(
                 )
                 nc.sync.dma_start(out_v[:, rows, c * CW : (c + 1) * CW], done[:, rows, :])
 
-        def finish_turned(c):
-            done = sb(f"done{c}", [P, PACK, CW], F32)
+        def multiply_turned(c):
             for wb in range(CW // P):
                 cols = slice(wb * P, (wb + 1) * P)
                 acc = bank(f"ot_ps{wb}", 2 + wb)
@@ -306,7 +305,12 @@ def tile_picked_deeporderpagem_none_p_kernel(
                     nc.tensor.matmul(
                         total[:, rows], prod[:, rows], ident[:], start=False, stop=b == last, is_transpose=True
                     )
-                nc.scalar.copy(done[:, :, cols], total[:].rearrange("p (b w) -> p b w", b=PACK))
+
+        def store_turned(c):
+            done = sb(f"done{c}", [P, PACK, CW], F32)
+            for wb in range(CW // P):
+                cols = slice(wb * P, (wb + 1) * P)
+                nc.scalar.copy(done[:, :, cols], totals[wb][:].rearrange("p (b w) -> p b w", b=PACK))
             nc.sync.dma_start(out_v[:, :, c * CW : (c + 1) * CW], done[:])
 
         for step in range(chunks + 2):
@@ -315,6 +319,8 @@ def tile_picked_deeporderpagem_none_p_kernel(
             if 1 <= step <= chunks:
                 quantize_z2(step - 1)
             if step == 1:
-                finish_turned(0)
+                multiply_turned(0)
+            if step == 3:
+                store_turned(0)
             if step >= 3:
                 finish(step - 2)

from contextlib import ExitStack

import concourse.mybir as mybir
from concourse.masks import make_identity

K, T, S, N, H, W, U = 512, 2048, 512, 512, 512, 256, 1024
FLOPS = 2 * K * H * S + 2 * H * H * S + 2 * H * N * U

F32 = mybir.dt.float32
BF16 = mybir.dt.bfloat16
I32 = mybir.dt.int32
U32 = mybir.dt.uint32
U16 = mybir.dt.uint16
U8 = mybir.dt.uint8
FP8X4 = mybir.dt.float8_e4m3fn_x4
ALU = mybir.AluOpType
COPY = mybir.ActivationFunctionType.Copy

P = 128
PACK = 4
LANES = 16
CH = 128
CW = 256
M_SPLIT = 80


def tile_picked_deeporderpagem_none_p_kernel(
    tc, x_words, x_scales, w1, w2, mem, w3, res, offs, n1, n2, n3, n4, out
):
    nc = tc.nc
    with ExitStack() as ctx:
        keep = ctx.enter_context(tc.tile_pool(name="keep", bufs=1))
        psum = ctx.enter_context(tc.psum_pool(name="psum", bufs=1))

        def sb(name, shape, dtype, tag=None):
            return keep.tile(shape, dtype, name=name, tag=tag or name, align_bytes=64)

        def bank(name, number):
            return psum.tile([P, 512], F32, name=name, tag=f"bank{number}")

        def load_list(name, src):
            tile = keep.tile(list(src.shape), U16, name=name, tag=name)
            nc.sync.dma_start(tile[:], src)
            return tile

        def load_weight(name, src):
            raw = sb(name, [P, PACK, 512], F32)
            nc.sync.dma_start(raw[:], src.rearrange("(p j) c -> p j c", j=PACK))
            return raw

        def quantize(codes, scales, values):
            nc.vector.quantize_mx(out=codes.bitcast(FP8X4), scales=scales, in_=values)

        def mx(dst, lhs, lhs_cols, rhs, rhs_cols):
            nc.tensor.matmul_mx(
                out=dst,
                lhsT=lhs[0][:, lhs_cols].bitcast(FP8X4),
                lhsT_scale=lhs[1][:, lhs_cols],
                rhs=rhs[0][:, rhs_cols].bitcast(FP8X4),
                rhs_scale=rhs[1][:, rhs_cols],
                start=True,
                stop=True,
            )

        def dealt(grouped, raw, m0, m1, base=0):
            dst = grouped[:].rearrange("p (t m j) -> p m t j", t=PACK, j=PACK)[:, m0:m1]
            src = raw[:].rearrange("p j (m t) -> p m t j", t=PACK)[:, m0 - base : m1 - base]
            return dst, src

        xs = sb("xs", [P, T], U8)
        nc.vector.memset(xs[:].bitcast(I32), 0)
        offs_t = load_list("offs_t", offs)
        n1_t = load_list("n1_t", n1)
        n2_t = load_list("n2_t", n2)
        n3_t = load_list("n3_t", n3)
        w1_v = w1.rearrange("(p j) c -> p j c", j=PACK)
        w1_raw = []
        for half in range(2):
            raw = sb(f"w1_raw{half}", [P, PACK, H // 2], F32)
            nc.sync.dma_start(raw[:], w1_v[:, :, half * (H // 2) : (half + 1) * (H // 2)])
            w1_raw.append(raw)
        xw = sb("xw", [P, T], U32)
        nc.sync.dma_start(xw[:].bitcast(I32), x_words[0].rearrange("p n r -> p (n r)").bitcast(I32))
        n4_t = load_list("n4_t", n4)
        for q in range(4):
            nc.scalar.dma_start(
                xs[32 * q : 32 * q + 4, :].bitcast(I32), x_scales[0, 4 * q : 4 * q + 4, :].bitcast(I32)
            )
        w2_raw = load_weight("w2_raw", w2)
        w3_raw = load_weight("w3_raw", w3)
        res_v = res.rearrange("(b p) u -> p b u", p=P)
        out_v = out.rearrange("(b p) u -> p b u", p=P)

        def load_res(c):
            halves = []
            for half in range(2):
                r = sb(f"res{c}_{half}", [P, 2, CW], F32)
                nc.sync.dma_start(r[:], res_v[:, 2 * half : 2 * half + 2, c * CW : (c + 1) * CW])
                halves.append(r)
            return halves

        res_t = [load_res(0)]
        mem_v = mem.rearrange("(p t) u -> p t u", t=PACK)
        page = []
        for t in range(PACK):
            pg = sb(f"page{t}", [P, U], F32)
            nc.sync.dma_start(pg[:], mem_v[:, t, :])
            page.append(pg)
        res_t.extend(load_res(c) for c in range(1, U // CW))
        ident = sb("ident", [P, P], F32)
        make_identity(nc, ident[:])

        x_sc = sb("x_sc", [P, S], U8)
        nc.vector.tensor_copy(x_sc[:], xs[:].indirect(offs_t[:]))
        w1_bf = sb("w1_bf", [P, PACK * H], BF16)
        nc.scalar.copy(*dealt(w1_bf, w1_raw[0], 0, P // 2))
        nc.scalar.copy(*dealt(w1_bf, w1_raw[1], P // 2, M_SPLIT, P // 2))
        nc.vector.tensor_copy(*dealt(w1_bf, w1_raw[1], M_SPLIT, P, P // 2))
        w1_q = (sb("w1_codes", [P, H], U32), sb("w1_scales", [P, H], U8))
        for c0, c1 in ((0, P), (P, 2 * P), (2 * P, H)):
            quantize(w1_q[0][:, c0:c1], w1_q[1][:, c0:c1], w1_bf[:, PACK * c0 : PACK * c1])
        x_cd = sb("x_cd", [P, S], U32)
        x_q = (x_cd, x_sc)
        y = [sb(f"y{t}", [P, S], F32) for t in range(PACK)]
        for half in range(2):
            cols = slice(half * W, (half + 1) * W)
            nc.vector.tensor_copy(x_cd[:, cols], xw[:].indirect(offs_t[:, half * W // LANES : (half + 1) * W // LANES]))
            acc = bank(f"y0_ps{half}", half)
            mx(acc[:, 0:W], w1_q, slice(0, P), x_q, cols)
            nc.scalar.copy(y[0][:, cols], acc[:, 0:W])
        for t in range(1, PACK):
            acc = bank(f"y_ps{t}", t + 1)
            mx(acc[:], w1_q, slice(t * P, (t + 1) * P), x_q, slice(0, S))
            nc.scalar.copy(y[t][:], acc[:])

        w2_bf = sb("w2_bf", [P, PACK * H], BF16)
        nc.scalar.copy(*dealt(w2_bf, w2_raw, 0, P))
        w3_bf = sb("w3_bf", [P, PACK * N], BF16)
        nc.scalar.copy(
            w3_bf[:].rearrange("p (c i j) -> p c j i", i=4, j=PACK),
            w3_raw[:].rearrange("p j (c i) -> p c j i", i=4),
        )

        totals = []
        for wb in range(CW // P):
            acc = bank(f"rt_ps{wb}", 4 + wb)
            for b in range(PACK):
                nc.tensor.transpose(
                    acc[:, b * P : (b + 1) * P], res_t[0][b // 2][:, b % 2, wb * P : (wb + 1) * P], ident[:]
                )
            turned = sb(f"res_turned{wb}", [P, N], F32)
            nc.scalar.copy(turned[:], acc[:])
            total = bank(f"os_ps{wb}", 6 + wb)
            for b in range(PACK):
                rows = slice(b * P, (b + 1) * P)
                nc.tensor.matmul(total[:, rows], turned[:, rows], ident[:], start=b == 0, stop=False, is_transpose=True)
            totals.append(total)

        last = PACK - 1
        pair = [sb(f"pair{g}", [P, 2, 2, W], F32) for g in range(2)]
        high = [sb(f"high{g}", [P, 2, W], F32) for g in range(2)]
        low = [sb(f"low{g}", [P, 2, W], F32) for g in range(2)]
        z = [sb(f"z{t}", [P, S], F32) for t in range(PACK)]
        z_bf = sb("z_bf", [P, S, PACK], BF16)

        def fetch(t, side):
            nc.vector.tensor_copy(pair[t // 2][:, side, t % 2, :], y[t][:].indirect((n1_t, n2_t)[side][:]))

        def order(g):
            nc.vector.tensor_tensor(high[g][:], pair[g][:, 0], pair[g][:, 1], ALU.max)
            nc.vector.tensor_tensor(low[g][:], pair[g][:, 0], pair[g][:, 1], ALU.min)

        def put_high(t):
            nc.vector.tensor_copy(z[t][:].indirect(n1_t[:]), high[t // 2][:, t % 2, :])

        def put_low(t):
            nc.vector.tensor_copy(z[t][:].indirect(n2_t[:]), low[t // 2][:, t % 2, :])
            if t < last:
                nc.scalar.copy(z_bf[:, :, t], z[t][:])

        for t in range(2):
            fetch(t, 0)
            fetch(t, 1)
        fetch(2, 0)
        order(0)
        fetch(2, 1)
        put_high(0)
        fetch(3, 0)
        put_low(0)
        fetch(3, 1)
        put_high(1)
        order(1)
        put_low(1)
        put_high(2)
        put_high(3)
        put_low(2)
        put_low(3)

        w2_q = (sb("w2_codes", [P, H], U32, tag="high1"), sb("w2_scales", [P, H], U8))
        quantize(w2_q[0][:], w2_q[1][:], w2_bf[:])
        w3_q = (sb("w3_codes", [P, N], U32, tag="low1"), sb("w3_scales", [P, N], U8))

        z_q = (sb("z_codes", [P, S], U32), sb("z_scales", [P, S], U8))

        def round_last(c0, c1):
            nc.scalar.copy(z_bf[:, c0:c1, last], z[last][:, c0:c1])

        def quantize_z(c0, c1):
            quantize(z_q[0][:, c0:c1], z_q[1][:, c0:c1], z_bf[:, c0:c1, :].rearrange("p c t -> p (c t)"))

        round_last(0, CH)
        quantize_z(0, CH)
        quantize(w3_q[0][:], w3_q[1][:], w3_bf[:])
        round_last(CH, 2 * CH)
        h_first = []
        for t in range(PACK):
            acc = bank(f"hf_ps{t}", t)
            mx(acc[:, 0:CH], w2_q, slice(t * P, (t + 1) * P), z_q, slice(0, CH))
            ht = sb(f"h_first{t}", [P, CH], F32)
            nc.scalar.copy(ht[:], acc[:, 0:CH])
            h_first.append(ht)
        round_last(2 * CH, 3 * CH)
        round_last(3 * CH, 4 * CH)

        def put(t, c0, c1, src):
            nc.vector.tensor_copy(page[t][:].indirect(n3_t[:, c0 // LANES : c1 // LANES]), src)

        put(0, 0, CH, h_first[0][:])
        quantize_z(CH, 2 * CH)
        put(1, 0, CH, h_first[1][:])
        quantize_z(2 * CH, S)
        put(2, 0, CH, h_first[2][:])
        put(3, 0, CH, h_first[3][:])
        h_rest = []
        for t in range(PACK):
            acc = bank(f"hr_ps{t}", (4 + t) % 6)
            mx(acc[:, CH : 2 * CH], w2_q, slice(t * P, (t + 1) * P), z_q, slice(CH, 2 * CH))
            mx(acc[:, 2 * CH : S], w2_q, slice(t * P, (t + 1) * P), z_q, slice(2 * CH, S))
            ht = sb(f"h_rest{t}", [P, S - CH], F32)
            nc.scalar.copy(ht[:], acc[:, CH:S])
            h_rest.append(ht)
        chunks = U // CW
        twice = [[sb(f"twice{t}_{c}", [P, CW], F32) for c in range(chunks)] for t in range(PACK)]

        def double(t, c):
            nc.scalar.activation(twice[t][c][:], page[t][:, c * CW : (c + 1) * CW], COPY, scale=2.0)

        for t in range(PACK):
            put(t, CH, S, h_rest[t][:])
            if t < 2:
                for c in range(chunks):
                    double(t, c)
        for c in range(chunks):
            double(2, c)
            double(3, c)

        diff = [None] * chunks
        z2_q = [None] * chunks

        def fetch_diff(c):
            diff[c] = sb(f"diff{c}", [P, PACK, CW], F32, tag=("h_rest2", "twice2_0")[c % 2])
            for t in range(PACK):
                nc.vector.tensor_tensor(
                    diff[c][:, t, :],
                    page[t][:].indirect(n4_t[:, c * CW // LANES : (c + 1) * CW // LANES]),
                    twice[t][c][:],
                    ALU.subtract,
                )

        def quantize_z2(c):
            z2_bf = sb(f"z2_bf{c}", [P, CW * PACK], BF16, tag=(None, None, "twice2_1", "prod_turned0")[c])
            nc.scalar.activation(
                z2_bf[:].rearrange("p (c i t) -> p c t i", i=4, t=PACK),
                diff[c][:].rearrange("p t (c i) -> p c t i", i=4),
                COPY,
                scale=-0.5,
            )
            behind = f"twice2_{c + 1}" if c + 1 < chunks else None
            z2_q[c] = (sb(f"z2_codes{c}", [P, CW], U32, tag=behind), sb(f"z2_scales{c}", [P, CW], U8))
            quantize(z2_q[c][0][:], z2_q[c][1][:], z2_bf[:])

        def finish(c):
            done = sb(f"done{c}", [P, PACK, CW], F32, tag=(None, "h_rest2", "twice2_0", None)[c])
            for half in range(2):
                acc = bank(f"o_ps{c}_{half}", ((), (3, 2), (4, 5), (0, 1))[c][half])
                for i in range(2):
                    b = 2 * half + i
                    mx(acc[:, i * CW : (i + 1) * CW], w3_q, slice(b * P, (b + 1) * P), z2_q[c], slice(0, CW))
                rows = slice(2 * half, 2 * half + 2)
                nc.vector.tensor_tensor(
                    done[:, rows, :], acc[:].rearrange("p (b w) -> p b w", b=2), res_t[c][half][:], ALU.add
                )
                nc.sync.dma_start(out_v[:, rows, c * CW : (c + 1) * CW], done[:, rows, :])

        def multiply_turned(c):
            for wb in range(CW // P):
                cols = slice(wb * P, (wb + 1) * P)
                acc = bank(f"ot_ps{wb}", 2 + wb)
                mx(acc[:], z2_q[c], cols, w3_q, slice(0, N))
                prod = sb(f"prod_turned{wb}", [P, N], F32)
                nc.scalar.copy(prod[:], acc[:])
                total = totals[wb]
                for b in range(PACK):
                    rows = slice(b * P, (b + 1) * P)
                    nc.tensor.matmul(
                        total[:, rows], prod[:, rows], ident[:], start=False, stop=b == last, is_transpose=True
                    )

        def store_turned(c):
            done = sb(f"done{c}", [P, PACK, CW], F32)
            for wb in range(CW // P):
                cols = slice(wb * P, (wb + 1) * P)
                nc.scalar.copy(done[:, :, cols], totals[wb][:].rearrange("p (b w) -> p b w", b=PACK))
            nc.sync.dma_start(out_v[:, :, c * CW : (c + 1) * CW], done[:])

        for step in range(chunks + 2):
            if step < chunks:
                fetch_diff(step)
            if 1 <= step <= chunks:
                quantize_z2(step - 1)
            if step == 1:
                multiply_turned(0)
            if step == 3:
                store_turned(0)
            if step >= 3:
                finish(step - 2)
